import numpy as np
import ml_dtypes


def mxq(x, axis, fmt="e4m3"):
    dtype, down = {"e4m3": (ml_dtypes.float8_e4m3fn, 7), "e5m2": (ml_dtypes.float8_e5m2, 14)}[fmt]
    v = np.moveaxis(np.asarray(x, np.float32).astype(ml_dtypes.bfloat16).astype(np.float64), axis, -1)
    blocks = v.reshape(v.shape[:-1] + (-1, 32))
    amax = np.abs(blocks).max(-1, keepdims=True)
    byte = np.maximum(np.where(amax > 0, np.frexp(amax)[1] - 1 + 127, 0) - down, 1)
    scale = np.exp2(byte - 127.0)
    codes = (blocks / scale).astype(np.float32).astype(dtype).astype(np.float64)
    return np.moveaxis((codes * scale).reshape(v.shape), -1, axis)


WIDE = False


def mx_kscale(k):
    if not WIDE:
        return np.ones(k)
    levels = np.array([10, -10, 5, -5, 0])
    if k % 512:
        return np.exp2(np.random.permutation(np.resize(levels, k // 32))).repeat(32)
    a = np.empty((k // 512, 16))
    for p in range(k // 512):
        a[p, :8] = np.random.permutation(np.resize(levels, 8))
        for g in range(8):
            far = levels[np.abs(levels - a[p, g]) >= 10]
            a[p, g + 8] = far[np.random.randint(len(far))]
    return np.exp2(a.ravel()).repeat(32)


def f64(x):
    return np.asarray(x).astype(np.float64)


def striped(idx):
    return np.tile(idx.reshape(-1, 16).T, (8, 1)).astype(np.uint16)


def unstriped(offs):
    return offs[:16].T.reshape(-1).astype(np.int64)


def striped8(idx):
    return np.concatenate([x.reshape(-1, 16).T for x in idx]).astype(np.uint16)


def runs(offs, k):
    lists = np.stack([offs[16 * r : 16 * r + 16].T.reshape(-1) for r in range(8)]).astype(np.int64)
    return lists[np.arange(k) % 512 // 64]


def pack_weight(w):
    k, n = w.shape
    w = f64(np.asarray(w, np.float32).astype(ml_dtypes.bfloat16)).reshape(k // 32, 32, n)
    amax = np.abs(w).max(1)
    byte = np.clip(np.where(amax > 0, np.frexp(amax)[1] - 1 + 127 - 7, 1), 1, 254)
    scaled = (w * np.exp2(127.0 - byte)[:, None, :]).reshape(k, n).astype(np.float32)
    words = np.ascontiguousarray(scaled.reshape(k // 512, 128, 4, n).transpose(0, 1, 3, 2)).astype(ml_dtypes.float8_e4m3fn).view(np.uint8)
    return words, np.ascontiguousarray(byte.astype(np.uint8).reshape(k // 512, 16, n))


def unpack_weight(words, scales):
    g, p, n, _ = words.shape
    vals = np.ascontiguousarray(words).view(ml_dtypes.float8_e4m3fn).astype(np.float64) * np.repeat(np.exp2(scales.astype(np.float64) - 127.0), 8, axis=1)[..., None]
    return vals.transpose(0, 1, 3, 2).reshape(g * 512, n)


def sigmoid(v):
    return 1.0 / (1.0 + np.exp(-np.maximum(v, -700.0)))


K, T, S, H, C = 512, 2048, 512, 512, 512


def setup_inputs():
    n = np.random.standard_normal
    s = mx_kscale(K)[:, None]
    packed_xT = pack_weight(n((K, T)) * s)
    return {
        "x_words": packed_xT[0],
        "x_scales": packed_xT[1],
        "w1": (n((K, H)) / np.sqrt(K) / s).astype(np.float32),
        "w2": (n((K, H)) / np.sqrt(K) / s).astype(np.float32),
        "sl": np.random.uniform(1.0, 2.0, (H, 1)).astype(np.float32),
        "th": (0.5 * n((H, 1))).astype(np.float32),
        "gs": (np.random.uniform(0.5, 1.5, (K, 1)) / s).astype(np.float32),
        "tau": np.random.uniform(0.3, 0.9, (C, 1)).astype(np.float32),
        "offs": striped(np.random.permutation(T)[:S]),
        "two": striped(np.random.permutation(T)[:S]),
        "n1": striped8(np.stack([np.random.permutation(S) for _ in range(8)])),
        "n2": striped8(np.stack([np.random.permutation(S) for _ in range(8)])),
        "cand": striped(np.random.permutation(T)[:C]),
        "n3": striped(np.random.permutation(S)),
        "n4": striped(np.random.permutation(S)),
    }


def reference(x_words, x_scales, w1, w2, sl, th, gs, tau, offs, two, n1, n2, cand, n3, n4):
    x_cand = unpack_weight(x_words, x_scales)[:, unstriped(cand)]
    xq = unpack_weight(x_words, x_scales)[:, unstriped(offs)]
    y = mxq(f64(w1), 0, "e4m3").T @ xq
    x_two = unpack_weight(x_words, x_scales)[:, unstriped(two)]
    d = mxq(f64(w2), 0, "e4m3").T @ x_two
    sg = sigmoid(f64(sl) * (d[np.arange(H)[:, None], runs(n1, H)] - f64(th)))
    z = f64(gs) * (np.maximum(y * sg, d[np.arange(H)[:, None], runs(n2, H)] - d))
    s = 0.0625 * ((x_cand.T @ mxq(z, 0, "e4m3")))
    top = s.max(axis=1, keepdims=True)
    ea = np.exp(f64(tau) * (s[:, unstriped(n3)] - top))
    ea2 = np.exp(f64(tau) * (s[:, unstriped(n4)] - top))
    return (ea * s[:, unstriped(n3)] + ea2 * s[:, unstriped(n4)]) / (ea + ea2 + 0.125)

@@ -1,0 +1,278 @@
+from contextlib import ExitStack
+
+import concourse.mybir as mybir
+
+K, T, S, H, C = 512, 2048, 512, 512, 512
+FLOPS = 2 * K * H * S * 2 + 2 * K * C * S
+
+F32 = mybir.dt.float32
+BF16 = mybir.dt.bfloat16
+I32 = mybir.dt.int32
+U32 = mybir.dt.uint32
+U16 = mybir.dt.uint16
+U8 = mybir.dt.uint8
+FP8X4 = mybir.dt.float8_e4m3fn_x4
+ALU = mybir.AluOpType
+ACT = mybir.ActivationFunctionType
+
+P = 128
+PACK = 4
+HALF = S // 2
+LIST_COLS = S // 16
+
+
+def halves(ap):
+    return ap.rearrange("p (a n) -> p a n", a=2)
+
+
+def swapped(ap):
+    return halves(ap)[:, ::-1, :]
+
+
+def twice(ap):
+    return ap.unsqueeze(1).to_broadcast([P, 2, ap.shape[1]])
+
+
+def tile_picked_twcmxbevo_none_p_kernel(
+    tc, x_words, x_scales, w1, w2, sl, th, gs, tau, offs, two, n1, n2, cand, n3, n4, out
+):
+    nc = tc.nc
+    with ExitStack() as ctx:
+        keep = ctx.enter_context(tc.tile_pool(name="keep", bufs=1))
+        work = ctx.enter_context(tc.tile_pool(name="work", bufs=3))
+        psum = ctx.enter_context(tc.psum_pool(name="psum", bufs=1))
+
+        def load_list(src, name):
+            lst = keep.tile([P, LIST_COLS], U16, name=name)
+            nc.sync.dma_start(lst[:], src)
+            return lst
+
+        def half_of(lst, h):
+            return lst[:, h * (LIST_COLS // 2) : (h + 1) * (LIST_COLS // 2)]
+
+        xs = keep.tile([P, T], U8, name="xs", align_bytes=64)
+        nc.vector.memset(xs[:].bitcast(I32), 0)
+        two_l = load_list(two, "two_l")
+        xs_in = keep.tile([P, T // 4], I32, name="xs_in")
+        for q in range(4):
+            nc.sync.dma_start(xs_in[32 * q : 32 * q + 4, :], x_scales[0, 4 * q : 4 * q + 4, :].bitcast(I32))
+        for q in range(4):
+            nc.vector.tensor_copy(xs[32 * q : 32 * q + 4, :].bitcast(I32), xs_in[32 * q : 32 * q + 4, :])
+        offs_l = load_list(offs, "offs_l")
+        cand_l = load_list(cand, "cand_l")
+        w2_raw = keep.tile([P, PACK, H], F32, name="w2_raw")
+        nc.sync.dma_start(w2_raw[:], w2.rearrange("(p j) c -> p j c", j=PACK))
+        xw = keep.tile([P, T], I32, name="xw", align_bytes=64)
+        nc.sync.dma_start(xw[:], x_words[0].rearrange("p n t -> p (n t)").bitcast(I32))
+        n1_l = load_list(n1, "n1_l")
+        n2_l = load_list(n2, "n2_l")
+        w1_raw = keep.tile([P, PACK, H], F32, name="w1_raw", tag="w1_raw")
+        nc.sync.dma_start(w1_raw[:], w1.rearrange("(p j) c -> p j c", j=PACK))
+        n3_l = load_list(n3, "n3_l")
+        n4_l = load_list(n4, "n4_l")
+
+        def load_rows(src, name, pattern):
+            col = keep.tile([P, PACK], F32, name=name)
+            nc.gpsimd.dma_start(col[:], src.rearrange(pattern, p=P))
+            return col
+
+        sl_c = load_rows(sl, "sl_c", "(p t) o -> p (t o)")
+        th_c = load_rows(th, "th_c", "(p t) o -> p (t o)")
+        gs_c = load_rows(gs, "gs_c", "(p t) o -> p (t o)")
+        with nc.allow_non_contiguous_dma(reason="one value a partition and block"):
+            tau_c = load_rows(tau, "tau_c", "(b p) o -> p (b o)")
+        sl_th = keep.tile([P, PACK], F32, name="sl_th")
+        nc.gpsimd.tensor_tensor(sl_th[:], sl_c[:], th_c[:], ALU.mult)
+        sg_bias = keep.tile([P, PACK], F32, name="sg_bias")
+        nc.gpsimd.tensor_scalar(sg_bias[:], sl_th[:], -1.0, 0.0, ALU.mult, ALU.add)
+        neg_tau = []
+        for b in range(PACK):
+            col = keep.tile([P, 1], F32, name=f"neg_tau{b}", tag=f"picked{b}")
+            nc.gpsimd.tensor_scalar(col[:], tau_c[:, b : b + 1], -1.0, 0.0, ALU.mult, ALU.add)
+            neg_tau.append(col)
+
+        def pick_scales(lst, name):
+            got = keep.tile([P, S], U8, name=name, align_bytes=64)
+            nc.vector.tensor_copy(got[:], xs[:].indirect(lst[:]))
+            return got
+
+        def pick_words(entries, name, tag):
+            got = keep.tile([P, 16 * entries.shape[1]], U32, name=name, tag=tag, align_bytes=64)
+            nc.vector.tensor_copy(got[:], xw[:].bitcast(U32).indirect(entries))
+            return got
+
+        def deal(raw, name, copy):
+            dealt = keep.tile([P, H * PACK], BF16, name=name, tag=name, align_bytes=64)
+            copy(
+                dealt[:].rearrange("p (t m j) -> p m j t", t=PACK, j=PACK),
+                raw[:].rearrange("p j (m t) -> p m j t", t=PACK),
+            )
+            return dealt
+
+        def quantize_weight(dealt, name):
+            codes = keep.tile([P, H], U32, name=name + "_codes", align_bytes=64)
+            scales = keep.tile([P, H], U8, name=name + "_scales", align_bytes=64)
+            step = H // 2
+            for c in range(0, H, step):
+                nc.vector.quantize_mx(
+                    out=codes[:, c : c + step].bitcast(FP8X4), scales=scales[:, c : c + step],
+                    in_=dealt[:, PACK * c : PACK * (c + step)],
+                )
+            return codes, scales
+
+        two_s = pick_scales(two_l, "two_s")
+        offs_s = pick_scales(offs_l, "offs_s")
+        cand_s = pick_scales(cand_l, "cand_s")
+        w2_dealt = deal(w2_raw, "w2_dealt", nc.scalar.copy)
+        w2_q, w2_s = quantize_weight(w2_dealt, "w2")
+        two_w = pick_words(two_l[:], "two_w", "two_w")
+
+        d_ps, d_sb = [], []
+        for t in range(PACK):
+            bank = psum.tile([P, S], F32, name=f"d_ps{t}")
+            cols = slice(t * P, (t + 1) * P)
+            nc.tensor.matmul_mx(
+                out=bank[:], lhsT=w2_q[:, cols].bitcast(FP8X4), lhsT_scale=w2_s[:, cols],
+                rhs=two_w[:].bitcast(FP8X4), rhs_scale=two_s[:], start=True, stop=True,
+            )
+            d_ps.append(bank)
+        offs_w = [pick_words(half_of(offs_l, h), f"offs_w{h}", tag) for h, tag in enumerate(("w2_dealt", "two_w"))]
+        w1_dealt = deal(w1_raw, "w1_dealt", nc.vector.tensor_copy)
+        w1_q, w1_s = quantize_weight(w1_dealt, "w1")
+
+        cand_w = [pick_words(half_of(cand_l, 0), "cand_w0", "w1_dealt")]
+
+        d_sb = []
+        for t in range(PACK):
+            rows = keep.tile([P, S], F32, name=f"d_sb{t}", tag=f"d_sb{t}" if t in [0,1,2,3] else "w1_raw")
+            copy = nc.vector.tensor_copy if t in [0,1,2,3] else nc.scalar.copy
+            copy(rows[:], d_ps[t][:])
+            d_sb.append(rows)
+
+        s_sb, larger = [], []
+        z_rows = keep.tile([P, PACK, S], BF16, name="z_rows")
+        for t in range(PACK):
+            cols = slice(t * P, (t + 1) * P)
+            y_ps = psum.tile([P, S], F32, name=f"y_ps{t}", tag=f"bank{t}")
+            for h in range(2):
+                hc = slice(h * HALF, (h + 1) * HALF)
+                nc.tensor.matmul_mx(
+                    out=y_ps[:, hc], lhsT=w1_q[:, cols].bitcast(FP8X4), lhsT_scale=w1_s[:, cols],
+                    rhs=offs_w[h][:].bitcast(FP8X4), rhs_scale=offs_s[:, hc], start=True, stop=True,
+                )
+            s_win = keep.tile([P, 2 * S], F32, name=f"s_win{t}")
+            s_sb.append(s_win)
+            sg = s_win[:, S:]
+            d_n2 = keep.tile([P, S], F32, name=f"d_n2{t}")
+            for h in range(2):
+                nc.scalar.activation(
+                    halves(sg)[:, h, :], d_sb[t][:].indirect(half_of(n1_l, h)), ACT.Sigmoid,
+                    bias=sg_bias[:, t : t + 1], scale=sl_c[:, t : t + 1],
+                )
+            for h in range(2):
+                if [t, h] in []:
+                    nc.vector.tensor_copy(halves(d_n2[:])[:, h, :], d_sb[t][:].indirect(half_of(n2_l, h)))
+                else:
+                    nc.scalar.activation(halves(d_n2[:])[:, h, :], d_sb[t][:].indirect(half_of(n2_l, h)), ACT.Copy)
+            gated = keep.tile([P, S], F32, name=f"gated{t}")
+            nc.vector.tensor_tensor(gated[:], y_ps[:], sg, ALU.mult)
+            diff = keep.tile([P, S], F32, name=f"diff{t}")
+            big = keep.tile([P, S], F32, name=f"larger{t}")
+            for part in [slice(0, S)] if t < PACK - 1 else [slice(0, HALF), slice(HALF, S)]:
+                nc.vector.tensor_tensor(diff[:, part], d_n2[:, part], d_ps[t][:, part], ALU.subtract)
+                nc.vector.tensor_tensor(big[:, part], gated[:, part], diff[:, part], ALU.max)
+                if t == PACK - 1:
+                    nc.vector.tensor_scalar(z_rows[:, t, part], big[:, part], gs_c[:, t : t + 1], None, ALU.mult)
+            larger.append(big)
+
+        for t in range(PACK - 1):
+            if t in [0,1,2]:
+                nc.scalar.activation(z_rows[:, t, :], larger[t][:], ACT.Copy, scale=gs_c[:, t : t + 1])
+            else:
+                nc.vector.tensor_scalar(z_rows[:, t, :], larger[t][:], gs_c[:, t : t + 1], None, ALU.mult)
+        z_q = keep.tile([P, S], U32, name="z_q", align_bytes=64)
+        z_s = keep.tile([P, S], U8, name="z_s", align_bytes=64)
+        for h, copy in enumerate((nc.scalar.copy, nc.vector.tensor_copy)):
+            hc = slice(h * HALF, (h + 1) * HALF)
+            z_dealt = keep.tile([P, HALF, PACK], BF16, name=f"z_dealt{h}", tag=f"z_dealt{h}", align_bytes=64)
+            copy(
+                z_dealt[:].rearrange("p (c i) t -> p c t i", i=4),
+                z_rows[:, :, hc].rearrange("p t (c i) -> p c t i", i=4),
+            )
+            nc.vector.quantize_mx(
+                out=z_q[:, hc].bitcast(FP8X4), scales=z_s[:, hc], in_=z_dealt[:].rearrange("p c t -> p (c t)")
+            )
+
+        ea_bias = keep.tile([P, PACK], F32, name="ea_bias")
+        for b in range(PACK):
+            cols = slice(b * P, (b + 1) * P)
+            if b == 2:
+                cand_w.append(pick_words(half_of(cand_l, 1), "cand_w1", "z_dealt1"))
+            bank = psum.tile([P, S], F32, name=f"s_ps{b}", tag=f"bank{b}")
+            nc.tensor.matmul_mx(
+                out=bank[:], lhsT=cand_w[b // 2][:, (b % 2) * P : (b % 2 + 1) * P].bitcast(FP8X4),
+                lhsT_scale=cand_s[:, cols],
+                rhs=z_q[:].bitcast(FP8X4), rhs_scale=z_s[:], start=True, stop=True,
+            )
+            if b < 2:
+                tops = keep.tile([P, PACK], F32, name=f"tops{b}", tag="tops")
+            top = tops[:, b : b + 1]
+            nc.vector.tensor_scalar(s_sb[b][:, :S], bank[:], 0.0625, None, ALU.mult, ALU.max, accum_out=top)
+            nc.vector.tensor_scalar(ea_bias[:, b : b + 1], top, neg_tau[b][:], None, ALU.mult)
+
+        def product(name, left, right, op):
+            got = work.tile(list(left.shape), F32, name=name)
+            nc.vector.tensor_tensor(got[:], left, right, op)
+            return got
+
+        def fold(name, src):
+            width = src.shape[1] // 2
+            return product(name, src[:, :width], src[:, width:], ALU.mult)
+
+        def unfold(name, parts, inv):
+            got = work.tile(list(parts.shape), F32, name=name)
+            nc.vector.tensor_tensor(halves(got[:]), swapped(parts), twice(inv), ALU.mult)
+            return got
+
+        for group in [[0],[1],[2],[3]]:
+            chain = [work.tile([P, len(group) * HALF], F32, name="den2")]
+            num2 = []
+            for i, b in enumerate(group):
+                ea = work.tile([P, S], F32, name="ea")
+                ea2 = work.tile([P, S], F32, name="ea2")
+                picked = keep.tile([P, 2, S], F32, name=f"picked{b}", tag=f"picked{b}")
+                s3, s4 = picked[:, 0, :], picked[:, 1, :]
+                for dst, lst in ((ea, n3_l), (ea2, n4_l)):
+                    nc.scalar.activation(
+                        dst[:], s_sb[b][:].indirect(lst[:]), ACT.Exp,
+                        bias=ea_bias[:, b : b + 1], scale=tau_c[:, b : b + 1],
+                    )
+                for dst, lst in ((s3, n3_l), (s4, n4_l)):
+                    nc.scalar.activation(dst, s_sb[b][:].indirect(lst[:]), ACT.Copy)
+                den = work.tile([P, S], F32, name="den", bufs=2)
+                nc.vector.scalar_tensor_tensor(den[:], ea[:], 0.125, ea2[:], ALU.add, ALU.add)
+                nc.vector.tensor_tensor(chain[0][:, i * HALF : (i + 1) * HALF], den[:, :HALF], den[:, HALF:], ALU.mult)
+                if b == group[-1]:
+                    while chain[-1].shape[1] > 64:
+                        chain.append(fold(f"fold{len(chain)}", chain[-1][:]))
+                    inv = work.tile(list(chain[-1].shape), F32, name="inv")
+                    nc.vector.reciprocal(inv[:], chain[-1][:])
+                    for level in range(len(chain) - 2, -1, -1):
+                        inv = unfold(f"unfold{level}", chain[level][:], inv[:])
+                p3 = product("p3", ea[:], s3, ALU.mult)
+                p4 = product("p4", ea2[:], s4, ALU.mult)
+                num = product("num", p3[:], p4[:], ALU.add)
+                crossed = work.tile([P, S], F32, name="crossed")
+                nc.vector.tensor_tensor(halves(crossed[:]), halves(num[:]), swapped(den[:]), ALU.mult)
+                num2.append(crossed)
+            for i, b in enumerate(group):
+                res = work.tile([P, S], F32, name="res")
+                inv_b = inv[:, i * HALF : (i + 1) * HALF]
+                if b < PACK - 1:
+                    nc.vector.tensor_tensor(halves(res[:]), halves(num2[i][:]), twice(inv_b), ALU.mult)
+                    nc.sync.dma_start(out[b * P : (b + 1) * P, :], res[:])
+                else:
+                    for h in range(2):
+                        hc = slice(h * HALF, (h + 1) * HALF)
+                        nc.vector.tensor_tensor(res[:, hc], num2[i][:, hc], inv_b, ALU.mult)
+                        nc.sync.dma_start(out[b * P : (b + 1) * P, hc], res[:, hc])

@@ -47,6 +47,11 @@ def tile_picked_twcmxbevo_none_p_kernel(
             nc.sync.dma_start(lst[:], src)
             return lst
 
+        def load_rows(src, name, pattern):
+            col = keep.tile([P, PACK], F32, name=name)
+            nc.sync.dma_start(col[:], src.rearrange(pattern, p=P))
+            return col
+
         def half_of(lst, h):
             return lst[:, h * (LIST_COLS // 2) : (h + 1) * (LIST_COLS // 2)]
 
@@ -64,32 +69,18 @@ def tile_picked_twcmxbevo_none_p_kernel(
         nc.sync.dma_start(w2_raw[:], w2.rearrange("(p j) c -> p j c", j=PACK))
         xw = keep.tile([P, T], I32, name="xw", align_bytes=64)
         nc.sync.dma_start(xw[:], x_words[0].rearrange("p n t -> p (n t)").bitcast(I32))
+        sl_c = load_rows(sl, "sl_c", "(p t) o -> p (t o)")
+        th_c = load_rows(th, "th_c", "(p t) o -> p (t o)")
         n1_l = load_list(n1, "n1_l")
         n2_l = load_list(n2, "n2_l")
         w1_raw = keep.tile([P, PACK, H], F32, name="w1_raw", tag="w1_raw")
         nc.sync.dma_start(w1_raw[:], w1.rearrange("(p j) c -> p j c", j=PACK))
+        gs_c = load_rows(gs, "gs_c", "(p t) o -> p (t o)")
         n3_l = load_list(n3, "n3_l")
         n4_l = load_list(n4, "n4_l")
 
-        def load_rows(src, name, pattern):
-            col = keep.tile([P, PACK], F32, name=name)
-            nc.gpsimd.dma_start(col[:], src.rearrange(pattern, p=P))
-            return col
-
-        sl_c = load_rows(sl, "sl_c", "(p t) o -> p (t o)")
-        th_c = load_rows(th, "th_c", "(p t) o -> p (t o)")
-        gs_c = load_rows(gs, "gs_c", "(p t) o -> p (t o)")
         with nc.allow_non_contiguous_dma(reason="one value a partition and block"):
             tau_c = load_rows(tau, "tau_c", "(b p) o -> p (b o)")
-        sl_th = keep.tile([P, PACK], F32, name="sl_th")
-        nc.gpsimd.tensor_tensor(sl_th[:], sl_c[:], th_c[:], ALU.mult)
-        sg_bias = keep.tile([P, PACK], F32, name="sg_bias")
-        nc.gpsimd.tensor_scalar(sg_bias[:], sl_th[:], -1.0, 0.0, ALU.mult, ALU.add)
-        neg_tau = []
-        for b in range(PACK):
-            col = keep.tile([P, 1], F32, name=f"neg_tau{b}", tag=f"picked{b}")
-            nc.gpsimd.tensor_scalar(col[:], tau_c[:, b : b + 1], -1.0, 0.0, ALU.mult, ALU.add)
-            neg_tau.append(col)
 
         def pick_scales(lst, name):
             got = keep.tile([P, S], U8, name=name, align_bytes=64)
@@ -101,12 +92,14 @@ def tile_picked_twcmxbevo_none_p_kernel(
             nc.vector.tensor_copy(got[:], xw[:].bitcast(U32).indirect(entries))
             return got
 
-        def deal(raw, name, copy):
+        def deal(shares, name):
             dealt = keep.tile([P, H * PACK], BF16, name=name, tag=name, align_bytes=64)
-            copy(
-                dealt[:].rearrange("p (t m j) -> p m j t", t=PACK, j=PACK),
-                raw[:].rearrange("p j (m t) -> p m j t", t=PACK),
-            )
+            view = dealt[:].rearrange("p (t m j) -> p m j t", t=PACK, j=PACK)
+            m0 = 0
+            for raw, copy in shares:
+                src = raw.rearrange("p j (m t) -> p m j t", t=PACK)
+                copy(view[:, m0 : m0 + src.shape[1]], src)
+                m0 = m0 + src.shape[1]
             return dealt
 
         def quantize_weight(dealt, name):
@@ -123,13 +116,15 @@ def tile_picked_twcmxbevo_none_p_kernel(
         two_s = pick_scales(two_l, "two_s")
         offs_s = pick_scales(offs_l, "offs_s")
         cand_s = pick_scales(cand_l, "cand_s")
-        w2_dealt = deal(w2_raw, "w2_dealt", nc.scalar.copy)
+        sg_bias = keep.tile([P, PACK], F32, name="sg_bias")
+        nc.vector.scalar_tensor_tensor(sg_bias[:], th_c[:], -1.0, sl_c[:], ALU.mult, ALU.mult)
+        w2_dealt = deal([(w2_raw[:], nc.scalar.copy)], "w2_dealt")
         w2_q, w2_s = quantize_weight(w2_dealt, "w2")
         two_w = pick_words(two_l[:], "two_w", "two_w")
 
         d_ps, d_sb = [], []
         for t in range(PACK):
-            bank = psum.tile([P, S], F32, name=f"d_ps{t}")
+            bank = psum.tile([P, S], F32, name=f"d_ps{t}", tag=f"low{t}")
             cols = slice(t * P, (t + 1) * P)
             nc.tensor.matmul_mx(
                 out=bank[:], lhsT=w2_q[:, cols].bitcast(FP8X4), lhsT_scale=w2_s[:, cols],
@@ -137,10 +132,10 @@ def tile_picked_twcmxbevo_none_p_kernel(
             )
             d_ps.append(bank)
         offs_w = [pick_words(half_of(offs_l, h), f"offs_w{h}", tag) for h, tag in enumerate(("w2_dealt", "two_w"))]
-        w1_dealt = deal(w1_raw, "w1_dealt", nc.vector.tensor_copy)
+        w1_dealt = deal([(w1_raw[:], nc.vector.tensor_copy)], "w1_dealt")
         w1_q, w1_s = quantize_weight(w1_dealt, "w1")
 
-        cand_w = [pick_words(half_of(cand_l, 0), "cand_w0", "w1_dealt")]
+        cand_w = pick_words(cand_l[:], "cand_w", "w1_dealt")
 
         d_sb = []
         for t in range(PACK):
@@ -150,6 +145,7 @@ def tile_picked_twcmxbevo_none_p_kernel(
             d_sb.append(rows)
 
         s_sb, larger = [], []
+        diffs = keep.tile([P, PACK, S], F32, name="diffs", tag="w1_raw")
         z_rows = keep.tile([P, PACK, S], BF16, name="z_rows")
         for t in range(PACK):
             cols = slice(t * P, (t + 1) * P)
@@ -176,7 +172,7 @@ def tile_picked_twcmxbevo_none_p_kernel(
                     nc.scalar.activation(halves(d_n2[:])[:, h, :], d_sb[t][:].indirect(half_of(n2_l, h)), ACT.Copy)
             gated = keep.tile([P, S], F32, name=f"gated{t}")
             nc.vector.tensor_tensor(gated[:], y_ps[:], sg, ALU.mult)
-            diff = keep.tile([P, S], F32, name=f"diff{t}")
+            diff = diffs[:, t, :]
             big = keep.tile([P, S], F32, name=f"larger{t}")
             for part in [slice(0, S)] if t < PACK - 1 else [slice(0, HALF), slice(HALF, S)]:
                 nc.vector.tensor_tensor(diff[:, part], d_n2[:, part], d_ps[t][:, part], ALU.subtract)
@@ -203,22 +199,29 @@ def tile_picked_twcmxbevo_none_p_kernel(
                 out=z_q[:, hc].bitcast(FP8X4), scales=z_s[:, hc], in_=z_dealt[:].rearrange("p c t -> p (c t)")
             )
 
+        neg_tau0 = keep.tile([P, 1], F32, name="neg_tau0", tag="picked0")
+        nc.vector.tensor_scalar(neg_tau0[:], tau_c[:, 0:1], -1.0, None, ALU.mult)
         ea_bias = keep.tile([P, PACK], F32, name="ea_bias")
         for b in range(PACK):
             cols = slice(b * P, (b + 1) * P)
-            if b == 2:
-                cand_w.append(pick_words(half_of(cand_l, 1), "cand_w1", "z_dealt1"))
             bank = psum.tile([P, S], F32, name=f"s_ps{b}", tag=f"bank{b}")
-            nc.tensor.matmul_mx(
-                out=bank[:], lhsT=cand_w[b // 2][:, (b % 2) * P : (b % 2 + 1) * P].bitcast(FP8X4),
-                lhsT_scale=cand_s[:, cols],
-                rhs=z_q[:].bitcast(FP8X4), rhs_scale=z_s[:], start=True, stop=True,
-            )
             if b < 2:
                 tops = keep.tile([P, PACK], F32, name=f"tops{b}", tag="tops")
-            top = tops[:, b : b + 1]
-            nc.vector.tensor_scalar(s_sb[b][:, :S], bank[:], 0.0625, None, ALU.mult, ALU.max, accum_out=top)
-            nc.vector.tensor_scalar(ea_bias[:, b : b + 1], top, neg_tau[b][:], None, ALU.mult)
+            parts = [slice(HALF, S), slice(0, HALF)] if b == 0 else [slice(0, S)]
+            for i, part in enumerate(parts):
+                piece = bank if i == 0 else psum.tile([P, S], F32, name="s_ps0_rest", tag="low0")
+                nc.tensor.matmul_mx(
+                    out=piece[:, part], lhsT=cand_w[:, cols].bitcast(FP8X4),
+                    lhsT_scale=cand_s[:, cols],
+                    rhs=z_q[:, part].bitcast(FP8X4), rhs_scale=z_s[:, part], start=True, stop=True,
+                )
+                nc.vector.tensor_scalar(
+                    s_sb[b][:, part], piece[:, part], 0.0625, None, ALU.mult, ALU.max, accum_out=tops[:, b + i : b + i + 1]
+                )
+            if b == 0:
+                nc.vector.tensor_scalar(ea_bias[:, 0:1], tops[:, 0:1], tops[:, 1:2], neg_tau0[:], ALU.max, ALU.mult)
+            else:
+                nc.vector.tensor_scalar(ea_bias[:, b : b + 1], tops[:, b : b + 1], tau_c[:, b : b + 1], -1.0, ALU.mult, ALU.mult)
 
         def product(name, left, right, op):
             got = work.tile(list(left.shape), F32, name=name)

@@ -92,18 +92,21 @@ def tile_picked_twcmxbevo_none_p_kernel(
             nc.vector.tensor_copy(got[:], xw[:].bitcast(U32).indirect(entries))
             return got
 
+        def pool_copy(dst, src):
+            nc.gpsimd.tensor_scalar(dst, src, 1.0, 0.0, ALU.mult, ALU.add)
+
         def deal(shares, name):
             dealt = keep.tile([P, H * PACK], BF16, name=name, tag=name, align_bytes=64)
-            view = dealt[:].rearrange("p (t m j) -> p m j t", t=PACK, j=PACK)
+            view = dealt[:].rearrange("p (t m j) -> p m t j", t=PACK, j=PACK)
             m0 = 0
             for raw, copy in shares:
-                src = raw.rearrange("p j (m t) -> p m j t", t=PACK)
+                src = raw.rearrange("p j (m t) -> p m t j", t=PACK)
                 copy(view[:, m0 : m0 + src.shape[1]], src)
                 m0 = m0 + src.shape[1]
             return dealt
 
         def quantize_weight(dealt, name):
-            codes = keep.tile([P, H], U32, name=name + "_codes", align_bytes=64)
+            codes = keep.tile([P, H], U32, name=name + "_codes", tag=name + "_codes", align_bytes=64)
             scales = keep.tile([P, H], U8, name=name + "_scales", align_bytes=64)
             step = H // 2
             for c in range(0, H, step):
@@ -132,10 +135,9 @@ def tile_picked_twcmxbevo_none_p_kernel(
             )
             d_ps.append(bank)
         offs_w = [pick_words(half_of(offs_l, h), f"offs_w{h}", tag) for h, tag in enumerate(("w2_dealt", "two_w"))]
-        w1_dealt = deal([(w1_raw[:], nc.vector.tensor_copy)], "w1_dealt")
+        w1_dealt = deal([(w1_raw[:], pool_copy)], "w1_dealt")
         w1_q, w1_s = quantize_weight(w1_dealt, "w1")
 
-        cand_w = pick_words(cand_l[:], "cand_w", "w1_dealt")
 
         d_sb = []
         for t in range(PACK):
@@ -144,6 +146,7 @@ def tile_picked_twcmxbevo_none_p_kernel(
             copy(rows[:], d_ps[t][:])
             d_sb.append(rows)
 
+        cand_w = pick_words(cand_l[:], "cand_w", "w2_codes")
         s_sb, larger = [], []
         diffs = keep.tile([P, PACK, S], F32, name="diffs", tag="w1_raw")
         z_rows = keep.tile([P, PACK, S], BF16, name="z_rows")
@@ -228,6 +231,11 @@ def tile_picked_twcmxbevo_none_p_kernel(
             nc.vector.tensor_tensor(got[:], left, right, op)
             return got
 
+        def numerator(num, p3, p4, ea, ea2, s3, s4, part):
+            nc.vector.tensor_tensor(p3[:, part], ea[:, part], s3[:, part], ALU.mult)
+            nc.vector.tensor_tensor(p4[:, part], ea2[:, part], s4[:, part], ALU.mult)
+            nc.vector.tensor_tensor(num[:, part], p3[:, part], p4[:, part], ALU.add)
+
         def fold(name, src):
             width = src.shape[1] // 2
             return product(name, src[:, :width], src[:, width:], ALU.mult)
@@ -245,15 +253,23 @@ def tile_picked_twcmxbevo_none_p_kernel(
                 ea2 = work.tile([P, S], F32, name="ea2")
                 picked = keep.tile([P, 2, S], F32, name=f"picked{b}", tag=f"picked{b}")
                 s3, s4 = picked[:, 0, :], picked[:, 1, :]
-                for dst, lst in ((ea, n3_l), (ea2, n4_l)):
-                    nc.scalar.activation(
-                        dst[:], s_sb[b][:].indirect(lst[:]), ACT.Exp,
-                        bias=ea_bias[:, b : b + 1], scale=tau_c[:, b : b + 1],
-                    )
-                for dst, lst in ((s3, n3_l), (s4, n4_l)):
-                    nc.scalar.activation(dst, s_sb[b][:].indirect(lst[:]), ACT.Copy)
                 den = work.tile([P, S], F32, name="den", bufs=2)
-                nc.vector.scalar_tensor_tensor(den[:], ea[:], 0.125, ea2[:], ALU.add, ALU.add)
+                p3 = work.tile([P, S], F32, name="p3")
+                p4 = work.tile([P, S], F32, name="p4")
+                num = work.tile([P, S], F32, name="num")
+                parts = [slice(0, HALF), slice(HALF, S)] if b == 0 else [slice(0, S)]
+                for part in parts:
+                    entries = slice(part.start // 16, part.stop // 16)
+                    for dst, lst in ((ea, n3_l), (ea2, n4_l)):
+                        nc.scalar.activation(
+                            dst[:, part], s_sb[b][:].indirect(lst[:, entries]), ACT.Exp,
+                            bias=ea_bias[:, b : b + 1], scale=tau_c[:, b : b + 1],
+                        )
+                    for dst, lst in ((s3, n3_l), (s4, n4_l)):
+                        nc.scalar.activation(dst[:, part], s_sb[b][:].indirect(lst[:, entries]), ACT.Copy)
+                    nc.vector.scalar_tensor_tensor(den[:, part], ea[:, part], 0.125, ea2[:, part], ALU.add, ALU.add)
+                    if part.stop < S:
+                        numerator(num, p3, p4, ea, ea2, s3, s4, part)
                 nc.vector.tensor_tensor(chain[0][:, i * HALF : (i + 1) * HALF], den[:, :HALF], den[:, HALF:], ALU.mult)
                 if b == group[-1]:
                     while chain[-1].shape[1] > 64:
@@ -262,9 +278,7 @@ def tile_picked_twcmxbevo_none_p_kernel(
                     nc.vector.reciprocal(inv[:], chain[-1][:])
                     for level in range(len(chain) - 2, -1, -1):
                         inv = unfold(f"unfold{level}", chain[level][:], inv[:])
-                p3 = product("p3", ea[:], s3, ALU.mult)
-                p4 = product("p4", ea2[:], s4, ALU.mult)
-                num = product("num", p3[:], p4[:], ALU.add)
+                numerator(num, p3, p4, ea, ea2, s3, s4, parts[-1])
                 crossed = work.tile([P, S], F32, name="crossed")
                 nc.vector.tensor_tensor(halves(crossed[:]), halves(num[:]), swapped(den[:]), ALU.mult)
                 num2.append(crossed)

from contextlib import ExitStack

import concourse.mybir as mybir

K, T, S, H, C = 512, 2048, 512, 512, 512
FLOPS = 2 * K * H * S * 2 + 2 * K * C * S

F32 = mybir.dt.float32
BF16 = mybir.dt.bfloat16
I32 = mybir.dt.int32
U32 = mybir.dt.uint32
U16 = mybir.dt.uint16
U8 = mybir.dt.uint8
FP8X4 = mybir.dt.float8_e4m3fn_x4
ALU = mybir.AluOpType
ACT = mybir.ActivationFunctionType

P = 128
PACK = 4
HALF = S // 2
LIST_COLS = S // 16


def halves(ap):
    return ap.rearrange("p (a n) -> p a n", a=2)


def swapped(ap):
    return halves(ap)[:, ::-1, :]


def twice(ap):
    return ap.unsqueeze(1).to_broadcast([P, 2, ap.shape[1]])


def tile_picked_twcmxbevo_none_p_kernel(
    tc, x_words, x_scales, w1, w2, sl, th, gs, tau, offs, two, n1, n2, cand, n3, n4, out
):
    nc = tc.nc
    with ExitStack() as ctx:
        keep = ctx.enter_context(tc.tile_pool(name="keep", bufs=1))
        work = ctx.enter_context(tc.tile_pool(name="work", bufs=3))
        psum = ctx.enter_context(tc.psum_pool(name="psum", bufs=1))

        def load_list(src, name):
            lst = keep.tile([P, LIST_COLS], U16, name=name)
            nc.sync.dma_start(lst[:], src)
            return lst

        def load_rows(src, name, pattern):
            col = keep.tile([P, PACK], F32, name=name)
            nc.sync.dma_start(col[:], src.rearrange(pattern, p=P))
            return col

        def half_of(lst, h):
            return lst[:, h * (LIST_COLS // 2) : (h + 1) * (LIST_COLS // 2)]

        xs = keep.tile([P, T], U8, name="xs", align_bytes=64)
        nc.vector.memset(xs[:].bitcast(I32), 0)
        two_l = load_list(two, "two_l")
        xs_in = keep.tile([P, T // 4], I32, name="xs_in")
        for q in range(4):
            nc.sync.dma_start(xs_in[32 * q : 32 * q + 4, :], x_scales[0, 4 * q : 4 * q + 4, :].bitcast(I32))
        for q in range(4):
            nc.vector.tensor_copy(xs[32 * q : 32 * q + 4, :].bitcast(I32), xs_in[32 * q : 32 * q + 4, :])
        offs_l = load_list(offs, "offs_l")
        cand_l = load_list(cand, "cand_l")
        w2_raw = keep.tile([P, PACK, H], F32, name="w2_raw")
        nc.sync.dma_start(w2_raw[:], w2.rearrange("(p j) c -> p j c", j=PACK))
        xw = keep.tile([P, T], I32, name="xw", align_bytes=64)
        nc.sync.dma_start(xw[:], x_words[0].rearrange("p n t -> p (n t)").bitcast(I32))
        sl_c = load_rows(sl, "sl_c", "(p t) o -> p (t o)")
        th_c = load_rows(th, "th_c", "(p t) o -> p (t o)")
        n1_l = load_list(n1, "n1_l")
        n2_l = load_list(n2, "n2_l")
        w1_raw = keep.tile([P, PACK, H], F32, name="w1_raw", tag="w1_raw")
        nc.sync.dma_start(w1_raw[:], w1.rearrange("(p j) c -> p j c", j=PACK))
        gs_c = load_rows(gs, "gs_c", "(p t) o -> p (t o)")
        n3_l = load_list(n3, "n3_l")
        n4_l = load_list(n4, "n4_l")

        with nc.allow_non_contiguous_dma(reason="one value a partition and block"):
            tau_c = load_rows(tau, "tau_c", "(b p) o -> p (b o)")

        def pick_scales(lst, name):
            got = keep.tile([P, S], U8, name=name, align_bytes=64)
            nc.vector.tensor_copy(got[:], xs[:].indirect(lst[:]))
            return got

        def pick_words(entries, name, tag):
            got = keep.tile([P, 16 * entries.shape[1]], U32, name=name, tag=tag, align_bytes=64)
            nc.vector.tensor_copy(got[:], xw[:].bitcast(U32).indirect(entries))
            return got

        def pool_copy(dst, src):
            nc.gpsimd.tensor_scalar(dst, src, 1.0, 0.0, ALU.mult, ALU.add)

        def deal(shares, name):
            dealt = keep.tile([P, H * PACK], BF16, name=name, tag=name, align_bytes=64)
            view = dealt[:].rearrange("p (t m j) -> p m t j", t=PACK, j=PACK)
            m0 = 0
            for raw, copy in shares:
                src = raw.rearrange("p j (m t) -> p m t j", t=PACK)
                copy(view[:, m0 : m0 + src.shape[1]], src)
                m0 = m0 + src.shape[1]
            return dealt

        def quantize_weight(dealt, name):
            codes = keep.tile([P, H], U32, name=name + "_codes", tag=name + "_codes", align_bytes=64)
            scales = keep.tile([P, H], U8, name=name + "_scales", align_bytes=64)
            step = H // 2
            for c in range(0, H, step):
                nc.vector.quantize_mx(
                    out=codes[:, c : c + step].bitcast(FP8X4), scales=scales[:, c : c + step],
                    in_=dealt[:, PACK * c : PACK * (c + step)],
                )
            return codes, scales

        two_s = pick_scales(two_l, "two_s")
        offs_s = pick_scales(offs_l, "offs_s")
        cand_s = pick_scales(cand_l, "cand_s")
        sg_bias = keep.tile([P, PACK], F32, name="sg_bias")
        nc.vector.scalar_tensor_tensor(sg_bias[:], th_c[:], -1.0, sl_c[:], ALU.mult, ALU.mult)
        w2_dealt = deal([(w2_raw[:], nc.scalar.copy)], "w2_dealt")
        w2_q, w2_s = quantize_weight(w2_dealt, "w2")
        two_w = pick_words(two_l[:], "two_w", "two_w")

        d_ps, d_sb = [], []
        for t in range(PACK):
            bank = psum.tile([P, S], F32, name=f"d_ps{t}", tag=f"low{t}")
            cols = slice(t * P, (t + 1) * P)
            nc.tensor.matmul_mx(
                out=bank[:], lhsT=w2_q[:, cols].bitcast(FP8X4), lhsT_scale=w2_s[:, cols],
                rhs=two_w[:].bitcast(FP8X4), rhs_scale=two_s[:], start=True, stop=True,
            )
            d_ps.append(bank)
        offs_w = [pick_words(half_of(offs_l, h), f"offs_w{h}", tag) for h, tag in enumerate(("w2_dealt", "two_w"))]
        w1_dealt = deal([(w1_raw[:], pool_copy)], "w1_dealt")
        w1_q, w1_s = quantize_weight(w1_dealt, "w1")


        d_sb = []
        for t in range(PACK):
            rows = keep.tile([P, S], F32, name=f"d_sb{t}", tag=f"d_sb{t}" if t in [0,1,2,3] else "w1_raw")
            copy = nc.vector.tensor_copy if t in [0,1,2,3] else nc.scalar.copy
            copy(rows[:], d_ps[t][:])
            d_sb.append(rows)

        cand_w = pick_words(cand_l[:], "cand_w", "w2_codes")
        s_sb, larger = [], []
        diffs = keep.tile([P, PACK, S], F32, name="diffs", tag="w1_raw")
        z_rows = keep.tile([P, PACK, S], BF16, name="z_rows")
        for t in range(PACK):
            cols = slice(t * P, (t + 1) * P)
            y_ps = psum.tile([P, S], F32, name=f"y_ps{t}", tag=f"bank{t}")
            for h in range(2):
                hc = slice(h * HALF, (h + 1) * HALF)
                nc.tensor.matmul_mx(
                    out=y_ps[:, hc], lhsT=w1_q[:, cols].bitcast(FP8X4), lhsT_scale=w1_s[:, cols],
                    rhs=offs_w[h][:].bitcast(FP8X4), rhs_scale=offs_s[:, hc], start=True, stop=True,
                )
            s_win = keep.tile([P, 2 * S], F32, name=f"s_win{t}")
            s_sb.append(s_win)
            sg = s_win[:, S:]
            d_n2 = keep.tile([P, S], F32, name=f"d_n2{t}")
            for h in range(2):
                nc.scalar.activation(
                    halves(sg)[:, h, :], d_sb[t][:].indirect(half_of(n1_l, h)), ACT.Sigmoid,
                    bias=sg_bias[:, t : t + 1], scale=sl_c[:, t : t + 1],
                )
            for h in range(2):
                if [t, h] in []:
                    nc.vector.tensor_copy(halves(d_n2[:])[:, h, :], d_sb[t][:].indirect(half_of(n2_l, h)))
                else:
                    nc.scalar.activation(halves(d_n2[:])[:, h, :], d_sb[t][:].indirect(half_of(n2_l, h)), ACT.Copy)
            gated = keep.tile([P, S], F32, name=f"gated{t}")
            nc.vector.tensor_tensor(gated[:], y_ps[:], sg, ALU.mult)
            diff = diffs[:, t, :]
            big = keep.tile([P, S], F32, name=f"larger{t}")
            for part in [slice(0, S)] if t < PACK - 1 else [slice(0, HALF), slice(HALF, S)]:
                nc.vector.tensor_tensor(diff[:, part], d_n2[:, part], d_ps[t][:, part], ALU.subtract)
                nc.vector.tensor_tensor(big[:, part], gated[:, part], diff[:, part], ALU.max)
                if t == PACK - 1:
                    nc.vector.tensor_scalar(z_rows[:, t, part], big[:, part], gs_c[:, t : t + 1], None, ALU.mult)
            larger.append(big)

        for t in range(PACK - 1):
            if t in [0,1,2]:
                nc.scalar.activation(z_rows[:, t, :], larger[t][:], ACT.Copy, scale=gs_c[:, t : t + 1])
            else:
                nc.vector.tensor_scalar(z_rows[:, t, :], larger[t][:], gs_c[:, t : t + 1], None, ALU.mult)
        z_q = keep.tile([P, S], U32, name="z_q", align_bytes=64)
        z_s = keep.tile([P, S], U8, name="z_s", align_bytes=64)
        for h, copy in enumerate((nc.scalar.copy, nc.vector.tensor_copy)):
            hc = slice(h * HALF, (h + 1) * HALF)
            z_dealt = keep.tile([P, HALF, PACK], BF16, name=f"z_dealt{h}", tag=f"z_dealt{h}", align_bytes=64)
            copy(
                z_dealt[:].rearrange("p (c i) t -> p c t i", i=4),
                z_rows[:, :, hc].rearrange("p t (c i) -> p c t i", i=4),
            )
            nc.vector.quantize_mx(
                out=z_q[:, hc].bitcast(FP8X4), scales=z_s[:, hc], in_=z_dealt[:].rearrange("p c t -> p (c t)")
            )

        neg_tau0 = keep.tile([P, 1], F32, name="neg_tau0", tag="picked0")
        nc.vector.tensor_scalar(neg_tau0[:], tau_c[:, 0:1], -1.0, None, ALU.mult)
        ea_bias = keep.tile([P, PACK], F32, name="ea_bias")
        for b in range(PACK):
            cols = slice(b * P, (b + 1) * P)
            bank = psum.tile([P, S], F32, name=f"s_ps{b}", tag=f"bank{b}")
            if b < 2:
                tops = keep.tile([P, PACK], F32, name=f"tops{b}", tag="tops")
            parts = [slice(HALF, S), slice(0, HALF)] if b == 0 else [slice(0, S)]
            for i, part in enumerate(parts):
                piece = bank if i == 0 else psum.tile([P, S], F32, name="s_ps0_rest", tag="low0")
                nc.tensor.matmul_mx(
                    out=piece[:, part], lhsT=cand_w[:, cols].bitcast(FP8X4),
                    lhsT_scale=cand_s[:, cols],
                    rhs=z_q[:, part].bitcast(FP8X4), rhs_scale=z_s[:, part], start=True, stop=True,
                )
                nc.vector.tensor_scalar(
                    s_sb[b][:, part], piece[:, part], 0.0625, None, ALU.mult, ALU.max, accum_out=tops[:, b + i : b + i + 1]
                )
            if b == 0:
                nc.vector.tensor_scalar(ea_bias[:, 0:1], tops[:, 0:1], tops[:, 1:2], neg_tau0[:], ALU.max, ALU.mult)
            else:
                nc.vector.tensor_scalar(ea_bias[:, b : b + 1], tops[:, b : b + 1], tau_c[:, b : b + 1], -1.0, ALU.mult, ALU.mult)

        def product(name, left, right, op):
            got = work.tile(list(left.shape), F32, name=name)
            nc.vector.tensor_tensor(got[:], left, right, op)
            return got

        def numerator(num, p3, p4, ea, ea2, s3, s4, part):
            nc.vector.tensor_tensor(p3[:, part], ea[:, part], s3[:, part], ALU.mult)
            nc.vector.tensor_tensor(p4[:, part], ea2[:, part], s4[:, part], ALU.mult)
            nc.vector.tensor_tensor(num[:, part], p3[:, part], p4[:, part], ALU.add)

        def fold(name, src):
            width = src.shape[1] // 2
            return product(name, src[:, :width], src[:, width:], ALU.mult)

        def unfold(name, parts, inv):
            got = work.tile(list(parts.shape), F32, name=name)
            nc.vector.tensor_tensor(halves(got[:]), swapped(parts), twice(inv), ALU.mult)
            return got

        for group in [[0],[1],[2],[3]]:
            chain = [work.tile([P, len(group) * HALF], F32, name="den2")]
            num2 = []
            for i, b in enumerate(group):
                ea = work.tile([P, S], F32, name="ea")
                ea2 = work.tile([P, S], F32, name="ea2")
                picked = keep.tile([P, 2, S], F32, name=f"picked{b}", tag=f"picked{b}")
                s3, s4 = picked[:, 0, :], picked[:, 1, :]
                den = work.tile([P, S], F32, name="den", bufs=2)
                p3 = work.tile([P, S], F32, name="p3")
                p4 = work.tile([P, S], F32, name="p4")
                num = work.tile([P, S], F32, name="num")
                parts = [slice(0, HALF), slice(HALF, S)] if b == 0 else [slice(0, S)]
                for part in parts:
                    entries = slice(part.start // 16, part.stop // 16)
                    for dst, lst in ((ea, n3_l), (ea2, n4_l)):
                        nc.scalar.activation(
                            dst[:, part], s_sb[b][:].indirect(lst[:, entries]), ACT.Exp,
                            bias=ea_bias[:, b : b + 1], scale=tau_c[:, b : b + 1],
                        )
                    for dst, lst in ((s3, n3_l), (s4, n4_l)):
                        nc.scalar.activation(dst[:, part], s_sb[b][:].indirect(lst[:, entries]), ACT.Copy)
                    nc.vector.scalar_tensor_tensor(den[:, part], ea[:, part], 0.125, ea2[:, part], ALU.add, ALU.add)
                    if part.stop < S:
                        numerator(num, p3, p4, ea, ea2, s3, s4, part)
                nc.vector.tensor_tensor(chain[0][:, i * HALF : (i + 1) * HALF], den[:, :HALF], den[:, HALF:], ALU.mult)
                if b == group[-1]:
                    while chain[-1].shape[1] > 64:
                        chain.append(fold(f"fold{len(chain)}", chain[-1][:]))
                    inv = work.tile(list(chain[-1].shape), F32, name="inv")
                    nc.vector.reciprocal(inv[:], chain[-1][:])
                    for level in range(len(chain) - 2, -1, -1):
                        inv = unfold(f"unfold{level}", chain[level][:], inv[:])
                numerator(num, p3, p4, ea, ea2, s3, s4, parts[-1])
                crossed = work.tile([P, S], F32, name="crossed")
                nc.vector.tensor_tensor(halves(crossed[:]), halves(num[:]), swapped(den[:]), ALU.mult)
                num2.append(crossed)
            for i, b in enumerate(group):
                res = work.tile([P, S], F32, name="res")
                inv_b = inv[:, i * HALF : (i + 1) * HALF]
                if b < PACK - 1:
                    nc.vector.tensor_tensor(halves(res[:]), halves(num2[i][:]), twice(inv_b), ALU.mult)
                    nc.sync.dma_start(out[b * P : (b + 1) * P, :], res[:])
                else:
                    for h in range(2):
                        hc = slice(h * HALF, (h + 1) * HALF)
                        nc.vector.tensor_tensor(res[:, hc], num2[i][:, hc], inv_b, ALU.mult)
                        nc.sync.dma_start(out[b * P : (b + 1) * P, hc], res[:, hc])
